import numpy as np
import ml_dtypes


def mxq(x, axis, fmt="e4m3"):
    dtype, down = {"e4m3": (ml_dtypes.float8_e4m3fn, 7), "e5m2": (ml_dtypes.float8_e5m2, 14)}[fmt]
    v = np.moveaxis(np.asarray(x, np.float32).astype(ml_dtypes.bfloat16).astype(np.float64), axis, -1)
    blocks = v.reshape(v.shape[:-1] + (-1, 32))
    amax = np.abs(blocks).max(-1, keepdims=True)
    byte = np.maximum(np.where(amax > 0, np.frexp(amax)[1] - 1 + 127, 0) - down, 1)
    scale = np.exp2(byte - 127.0)
    codes = (blocks / scale).astype(np.float32).astype(dtype).astype(np.float64)
    return np.moveaxis((codes * scale).reshape(v.shape), -1, axis)


WIDE = False


def mx_kscale(k):
    if not WIDE:
        return np.ones(k)
    levels = np.array([10, -10, 5, -5, 0])
    if k % 512:
        return np.exp2(np.random.permutation(np.resize(levels, k // 32))).repeat(32)
    a = np.empty((k // 512, 16))
    for p in range(k // 512):
        a[p, :8] = np.random.permutation(np.resize(levels, 8))
        for g in range(8):
            far = levels[np.abs(levels - a[p, g]) >= 10]
            a[p, g + 8] = far[np.random.randint(len(far))]
    return np.exp2(a.ravel()).repeat(32)


BF16 = ml_dtypes.bfloat16


def bf(x):
    return np.asarray(x, np.float32).astype(BF16)


def f64(x):
    return np.asarray(x).astype(np.float64)


E2M1 = np.array([0.0, 0.5, 1.0, 1.5, 2.0, 3.0, 4.0, 6.0, -0.0, -0.5, -1.0, -1.5, -2.0, -3.0, -4.0, -6.0])


def pack_weight(w, fmt):
    k, n = w.shape
    w = f64(bf(w)).reshape(k // 32, 32, n)
    amax = np.abs(w).max(1)
    if fmt == "e4m3":
        byte = np.frexp(amax)[1] - 1 + 127 - 7
    else:
        mant, ex = np.frexp(amax / 6.0)
        byte = np.where(mant > 0.5, ex, ex - 1) + 127
    byte = np.clip(np.where(amax > 0, byte, 1), 1, 254)
    scaled = (w * np.exp2(127.0 - byte)[:, None, :]).reshape(k, n).astype(np.float32)
    by_word = np.ascontiguousarray(scaled.reshape(k // 512, 128, 4, n).transpose(0, 1, 3, 2))
    if fmt == "e4m3":
        words = by_word.astype(ml_dtypes.float8_e4m3fn).view(np.uint8)
    else:
        c = by_word.astype(ml_dtypes.float4_e2m1fn).view(np.uint8) & 0xF
        words = c[..., 0::2] | (c[..., 1::2] << 4)
    return np.ascontiguousarray(words), np.ascontiguousarray(byte.astype(np.uint8).reshape(k // 512, 16, n))


def unpack_weight(words, scales, fmt):
    g, p, n, _ = words.shape
    if fmt == "e4m3":
        vals = np.ascontiguousarray(words).view(ml_dtypes.float8_e4m3fn).astype(np.float64)
    else:
        nib = np.empty((g, p, n, 4), np.uint8)
        nib[..., 0::2] = words & 0xF
        nib[..., 1::2] = words >> 4
        vals = E2M1[nib]
    vals = vals * np.repeat(np.exp2(scales.astype(np.float64) - 127.0), 8, axis=1)[..., None]
    return vals.transpose(0, 1, 3, 2).reshape(g * 512, n)
def pack4(w):
    words, scales = pack_weight(w, "e2m1")
    return words.reshape(words.shape[0], 128, -1), scales


def unpack4(words, scales):
    return unpack_weight(words.reshape(words.shape[0], 128, -1, 2), scales, "e2m1")


def planes(Y):
    n, m = Y.shape
    b = f64(bf(Y)).reshape(n // 32, 32, m)
    amax = np.abs(b).max(1)
    byte = np.clip(np.where(amax > 0, np.frexp(amax)[1] - 1 + 127 - 7, 1), 1, 254)
    codes = (b * np.exp2(127.0 - byte)[:, None, :]).reshape(n, m).astype(np.float32).astype(ml_dtypes.float8_e4m3fn).view(np.uint8)
    words = codes.reshape(n // 512, 128, 4, m).transpose(0, 1, 3, 2)
    return np.ascontiguousarray(words), np.ascontiguousarray(byte.astype(np.uint8).reshape(n // 512, 16, m))


M, K, H, N = 2048, 1024, 1536, 512
WIDTH = 4.0

def setup_inputs():
    s = mx_kscale(K)
    t = mx_kscale(H)
    x = np.random.randn(M, K) * np.exp(0.4 * np.random.randn(M, 1)) * s
    filters = np.random.randn(K, H) / np.sqrt(K) / s[:, None] * t
    offset = 0.5 * np.random.randn(H) * t
    dist = np.abs(np.arange(H)[:, None] - np.arange(N) * (H / N))
    smooth = (1 + dist / WIDTH) ** -1.5 * np.exp(0.6 * np.random.randn(H, N))
    smooth = smooth / smooth.sum(axis=0) / t[:, None]
    filt_words, filt_scales = pack4(filters)
    smooth_words, smooth_scales = pack4(smooth)
    base = 0.2 * np.exp(0.5 * np.random.randn(N))
    gain = np.exp(0.8 * np.random.randn(N))
    return {"x": bf(x), "filt_words": filt_words, "filt_scales": filt_scales, "offset": bf(offset),
            "smooth_words": smooth_words, "smooth_scales": smooth_scales, "base": bf(base), "gain": bf(gain)}

def reference(x, filt_words, filt_scales, offset, smooth_words, smooth_scales, base, gain):
    F = unpack4(filt_words, filt_scales)
    S = unpack4(smooth_words, smooth_scales)
    z = mxq(f64(x), 1, "e4m3") @ F
    r = np.abs(z + f64(offset))
    e = mxq(r, 1, "e4m3") @ S
    y = np.sqrt(e + f64(base)) * f64(gain)
    Y = y.T
    words, scales = planes(Y)
    return y, words, scales

@@ -1,0 +1,319 @@
+from contextlib import ExitStack
+
+import concourse.mybir as mybir
+from concourse.masks import make_identity
+
+M, K, H, N = 2048, 1024, 1536, 512
+FLOPS = 2 * M * K * H + 2 * M * H * N
+
+F32 = mybir.dt.float32
+BF16 = mybir.dt.bfloat16
+I32 = mybir.dt.int32
+U32 = mybir.dt.uint32
+U8 = mybir.dt.uint8
+FP8X4 = mybir.dt.float8_e4m3fn_x4
+FP4X4 = mybir.dt.float4_e2m1fn_x4
+ACT = mybir.ActivationFunctionType
+ALU = mybir.AluOpType
+
+P = 128
+PACK = 4
+PASS = P * PACK
+GROUP = 512
+GROUPS = M // GROUP
+TILES = GROUP // P
+K_PASSES = K // PASS
+H_PASSES = H // PASS
+BANKS = 8
+RUN = 4
+
+
+def tile_ecg_rectified_band_features_h1_kernel(
+    tc, x, filt_words, filt_scales, offset, smooth_words, smooth_scales, base, gain, out_0, out_1, out_2
+):
+    nc = tc.nc
+    with ExitStack() as ctx:
+        keep = ctx.enter_context(tc.tile_pool(name="keep", bufs=1))
+        work = ctx.enter_context(tc.tile_pool(name="work", bufs=3))
+        psum = ctx.enter_context(tc.psum_pool(name="psum", bufs=1))
+        ctx.enter_context(tc.manual_schedule())
+
+        banks_taken = []
+
+        def next_bank():
+            index = len(banks_taken) % BANKS
+            bank = psum.tile([P, GROUP], F32, name="bank%d" % index, tag="bank%d" % index)
+            banks_taken.append(index)
+            return bank
+
+        f_scales_raw = keep.tile([P, K_PASSES, H], U8, align_bytes=64)
+        s_scales_raw = keep.tile([P, H_PASSES, N], U8, align_bytes=64)
+        nc.vector.memset(f_scales_raw[:].bitcast(I32), 0)
+        nc.vector.memset(s_scales_raw[:].bitcast(I32), 0)
+        ident = keep.tile([P, P], F32)
+        make_identity(nc, ident[:])
+        warm_in = keep.tile([P, 1], F32)
+        warm_out = keep.tile([P, 1], F32)
+        nc.vector.memset(warm_in[:], 1.0)
+        nc.scalar.activation(out=warm_out[:], in_=warm_in[:], func=ACT.Sqrt)
+
+        def load_scale_rows(tile, rows):
+            for q in range(4):
+                nc.sync.dma_start(
+                    out=tile[32 * q : 32 * q + 4, :, :].bitcast(I32),
+                    in_=rows[:, 4 * q : 4 * q + 4, :].rearrange("g r n -> r g n").bitcast(I32),
+                )
+
+        f_words_raw = {}
+
+        def load_f_words(hg):
+            raw = keep.tile([P, K_PASSES, 2 * PASS], U8, name="f_raw%d" % hg, align_bytes=64)
+            nc.sync.dma_start(
+                out=raw[:].bitcast(I32),
+                in_=filt_words[:, :, 2 * PASS * hg : 2 * PASS * (hg + 1)].rearrange("g p c -> p g c").bitcast(I32),
+            )
+            f_words_raw[hg] = raw
+
+        x_rows = {}
+
+        def load_x(first, count):
+            rows = keep.tile([P, count, K], BF16, name="x%d" % first, align_bytes=64)
+            nc.sync.dma_start(
+                out=rows[:], in_=x[P * first : P * (first + count), :].rearrange("(a p) k -> p a k", p=P)
+            )
+            for a in range(count):
+                x_rows[first + a] = rows[:, a, :]
+
+        def load_per_slot(vec, passes, name):
+            tile = keep.tile([P, passes, PACK], BF16, name=name)
+            nc.sync.dma_start(out=tile[:], in_=vec.rearrange("(g p t) -> p g t", p=P, t=PACK))
+            return tile
+
+        load_x(0, 1)
+        load_x(1, 1)
+        load_f_words(0)
+        load_scale_rows(f_scales_raw, filt_scales)
+        load_x(2, 2)
+        offset_sb = load_per_slot(offset, H_PASSES, "offset_sb")
+        load_f_words(1)
+        load_f_words(2)
+        load_x(4, 4)
+        s_words_raw = keep.tile([P, H_PASSES, 2 * N], U8, align_bytes=64)
+        nc.sync.dma_start(
+            out=s_words_raw[:].bitcast(I32), in_=smooth_words.rearrange("g p c -> p g c").bitcast(I32)
+        )
+        load_scale_rows(s_scales_raw, smooth_scales)
+        base_sb = load_per_slot(base, 1, "base_sb")
+        gain_sb = load_per_slot(gain, 1, "gain_sb")
+        load_x(8, 4)
+        load_x(12, 4)
+
+        def sort_columns(words_raw, scales_raw, passes, name):
+            words = keep.tile([P, PACK, passes, 2 * P], U8, name=name + "_words", align_bytes=64)
+            scales = keep.tile([P, PACK, passes, P], U8, name=name + "_scales", align_bytes=64)
+            nc.vector.tensor_copy(
+                out=words[:].rearrange("p t g (m b) -> p t g m b", b=2),
+                in_=words_raw.rearrange("p g (m t b) -> p t g m b", t=PACK, b=2),
+            )
+            nc.vector.tensor_copy(out=scales[:], in_=scales_raw.rearrange("p g (m t) -> p t g m", t=PACK))
+            return words, scales
+
+        f_sorted = {}
+
+        def sort_f(hg):
+            f_sorted[hg] = sort_columns(
+                f_words_raw[hg][:], f_scales_raw[:, :, PASS * hg : PASS * (hg + 1)], K_PASSES, "f%d" % hg
+            )
+
+        x_grouped = {}
+        x_mx = {}
+
+        def transpose_x(j):
+            for a in range(TILES):
+                words = x_rows[TILES * j + a].bitcast(F32)
+                bank = next_bank()
+                quarters = bank[:].rearrange("p (g u r) -> p g u r", g=K_PASSES, u=2)
+                for g in range(K_PASSES):
+                    for u in range(2):
+                        nc.tensor.transpose(
+                            quarters[:, g, u, :], words[:, 256 * g + u : 256 * (g + 1) : 2], ident[:]
+                        )
+                if a % 2 == 0:
+                    half = work.tile([P, K_PASSES, 2 * P, 2], F32, name="x_half", bufs=4, align_bytes=64)
+                    x_grouped[j, a // 2] = half
+                nc.scalar.copy(
+                    out=half[:, :, P * (a % 2) : P * (a % 2 + 1), :], in_=quarters.rearrange("p g u r -> p g r u")
+                )
+
+        def quantize_x(j):
+            codes = work.tile([P, K_PASSES, GROUP], U32, name="x_codes", bufs=2, align_bytes=64)
+            scales = work.tile([P, K_PASSES, GROUP], U8, name="x_scales", bufs=2, align_bytes=64)
+            for h in range(2):
+                cols = slice(2 * P * h, 2 * P * (h + 1))
+                for g in range(K_PASSES):
+                    nc.vector.quantize_mx(
+                        out=codes[:, g, cols].bitcast(FP8X4),
+                        scales=scales[:, g, cols],
+                        in_=x_grouped[j, h][:, g, :, :].rearrange("p r u -> p (r u)").bitcast(BF16),
+                    )
+            x_mx[j] = (codes, scales)
+
+        r_rows = {}
+        r_grouped = {}
+        r_mx = {}
+
+        def filter_bank(j, hg):
+            words, w_scales = f_sorted[hg]
+            codes, scales = x_mx[j]
+            rows = work.tile([P, PACK, GROUP], BF16, name="r_rows", align_bytes=64)
+            for t in range(PACK):
+                bank = next_bank()
+                for g in range(K_PASSES):
+                    nc.tensor.matmul_mx(
+                        out=bank[:],
+                        lhsT=words[:, t, g, :].bitcast(FP4X4),
+                        lhsT_scale=w_scales[:, t, g, :],
+                        rhs=codes[:, g, :].bitcast(FP8X4),
+                        rhs_scale=scales[:, g, :],
+                        start=(g == 0),
+                        stop=(g == K_PASSES - 1),
+                    )
+                nc.scalar.activation(
+                    out=rows[:, t, :], in_=bank[:], func=ACT.Abs, bias=offset_sb[:, hg, t : t + 1]
+                )
+            r_rows[j, hg] = rows
+
+        def interleave(rows, name):
+            grouped = work.tile([P, GROUP, PACK], BF16, name=name, align_bytes=64)
+            nc.vector.tensor_copy(
+                out=grouped[:].rearrange("p (c i) t -> p c t i", i=RUN),
+                in_=rows[:].rearrange("p t (c i) -> p c t i", i=RUN),
+            )
+            return grouped
+
+        def interleave_r(j, hg):
+            r_grouped[j, hg] = interleave(r_rows[j, hg], "r_grouped")
+
+        def quantize_r(j, hg):
+            codes = work.tile([P, GROUP], U32, name="r_codes", bufs=4, align_bytes=64)
+            scales = work.tile([P, GROUP], U8, name="r_scales", bufs=4, align_bytes=64)
+            nc.vector.quantize_mx(
+                out=codes[:].bitcast(FP8X4),
+                scales=scales[:],
+                in_=r_grouped[j, hg][:].rearrange("p c t -> p (c t)"),
+            )
+            r_mx[j, hg] = (codes, scales)
+
+        e_banks = {}
+
+        def smooth(j):
+            words, w_scales = s_sorted[0]
+            banks = [next_bank() for t in range(PACK)]
+            for hg in range(H_PASSES):
+                codes, scales = r_mx[j, hg]
+                for t in range(PACK):
+                    nc.tensor.matmul_mx(
+                        out=banks[t][:],
+                        lhsT=words[:, t, hg, :].bitcast(FP4X4),
+                        lhsT_scale=w_scales[:, t, hg, :],
+                        rhs=codes[:].bitcast(FP8X4),
+                        rhs_scale=scales[:],
+                        start=(hg == 0),
+                        stop=(hg == H_PASSES - 1),
+                    )
+            e_banks[j] = banks
+
+        y_rows = {}
+        y_scales = keep.tile([P, M], U8, align_bytes=64)
+
+        def features(j):
+            root = work.tile([P, PACK, GROUP], F32, name="root", bufs=2)
+            rows = work.tile([P, PACK, GROUP], F32, name="y_rows", bufs=2)
+            for t in range(PACK):
+                nc.scalar.activation(
+                    out=root[:, t, :], in_=e_banks[j][t][:], func=ACT.Sqrt, bias=base_sb[:, 0, t : t + 1]
+                )
+                nc.vector.tensor_scalar(
+                    out=rows[:, t, :], in0=root[:, t, :], scalar1=gain_sb[:, 0, t : t + 1], scalar2=None, op0=ALU.mult
+                )
+            y_rows[j] = rows
+
+        def planes(j):
+            cols = slice(GROUP * j, GROUP * (j + 1))
+            grouped = interleave(y_rows[j], "y_grouped")
+            codes = work.tile([P, GROUP], U32, name="y_codes", bufs=2, align_bytes=64)
+            nc.vector.quantize_mx(
+                out=codes[:].bitcast(FP8X4), scales=y_scales[:, cols], in_=grouped[:].rearrange("p c t -> p (c t)")
+            )
+            nc.sync.dma_start(
+                out=out_1[0, :, cols, :].rearrange("p m t -> p (m t)").bitcast(I32), in_=codes[:].bitcast(I32)
+            )
+
+        def store_scale_rows(cols):
+            for q in range(4):
+                nc.sync.dma_start(
+                    out=out_2[0, 4 * q : 4 * q + 4, cols].bitcast(I32),
+                    in_=y_scales[32 * q : 32 * q + 4, cols].bitcast(I32),
+                )
+
+        y_banks = {}
+
+        def transpose_y(j):
+            banks = [next_bank() for a in range(TILES)]
+            for a in range(TILES):
+                for t in range(PACK):
+                    nc.tensor.transpose(
+                        banks[a][:, P * t : P * (t + 1)], y_rows[j][:, t, P * a : P * (a + 1)], ident[:]
+                    )
+            y_banks[j] = banks
+
+        def store_y(j, copies):
+            for a in range(TILES):
+                result = work.tile([P, N], F32, name="y_out", bufs=4)
+                copies[a](
+                    out=result[:].rearrange("p (m t) -> p m t", t=PACK),
+                    in_=y_banks[j][a][:].rearrange("p (t m) -> p m t", t=PACK),
+                )
+                row0 = GROUP * j + P * a
+                nc.sync.dma_start(out=out_0[row0 : row0 + P, :], in_=result[:])
+
+        on_vector = [nc.vector.tensor_copy] * TILES
+        shared = [nc.vector.tensor_copy, nc.scalar.copy] * (TILES // 2)
+        s_sorted = []
+        transpose_x(0)
+        sort_f(0)
+        quantize_x(0)
+        sort_f(1)
+        sort_f(2)
+        last = GROUPS - 1
+        for j in range(GROUPS):
+            filter_bank(j, 0)
+            filter_bank(j, 1)
+            interleave_r(j, 0)
+            if j == 0:
+                s_sorted.append(sort_columns(s_words_raw[:], s_scales_raw[:], H_PASSES, "s"))
+            elif j < last:
+                transpose_y(j - 1)
+                store_y(j - 1, on_vector)
+            filter_bank(j, 2)
+            quantize_r(j, 0)
+            interleave_r(j, 1)
+            if j < last:
+                transpose_x(j + 1)
+            else:
+                transpose_y(j - 1)
+            interleave_r(j, 2)
+            quantize_r(j, 1)
+            quantize_r(j, 2)
+            if j == last:
+                store_y(j - 1, on_vector)
+                store_scale_rows(slice(0, GROUP * last))
+            smooth(j)
+            if j < last:
+                quantize_x(j + 1)
+            features(j)
+            if j == last:
+                transpose_y(j)
+            planes(j)
+        store_y(last, [nc.scalar.copy] * TILES)
+        store_scale_rows(slice(GROUP * last, M))

@@ -46,10 +46,12 @@ def tile_ecg_rectified_band_features_h1_kernel(
             banks_taken.append(index)
             return bank
 
-        f_scales_raw = keep.tile([P, K_PASSES, H], U8, align_bytes=64)
+        f_scales_first = keep.tile([P, K_PASSES, PASS], U8, align_bytes=64)
+        f_scales_rest = keep.tile([P, K_PASSES, H - PASS], U8, align_bytes=64)
         s_scales_raw = keep.tile([P, H_PASSES, N], U8, align_bytes=64)
-        nc.vector.memset(f_scales_raw[:].bitcast(I32), 0)
-        nc.vector.memset(s_scales_raw[:].bitcast(I32), 0)
+        for plane in (f_scales_first, f_scales_rest, s_scales_raw):
+            nc.vector.memset(plane[:].bitcast(I32), 0)
+        f_scales_raw = [f_scales_first[:], f_scales_rest[:, :, :PASS], f_scales_rest[:, :, PASS:]]
         ident = keep.tile([P, P], F32)
         make_identity(nc, ident[:])
         warm_in = keep.tile([P, 1], F32)
@@ -57,11 +59,11 @@ def tile_ecg_rectified_band_features_h1_kernel(
         nc.vector.memset(warm_in[:], 1.0)
         nc.scalar.activation(out=warm_out[:], in_=warm_in[:], func=ACT.Sqrt)
 
-        def load_scale_rows(tile, rows):
+        def load_scale_rows(tile, rows, cols):
             for q in range(4):
                 nc.sync.dma_start(
                     out=tile[32 * q : 32 * q + 4, :, :].bitcast(I32),
-                    in_=rows[:, 4 * q : 4 * q + 4, :].rearrange("g r n -> r g n").bitcast(I32),
+                    in_=rows[:, 4 * q : 4 * q + 4, cols].rearrange("g r n -> r g n").bitcast(I32),
                 )
 
         f_words_raw = {}
@@ -91,46 +93,55 @@ def tile_ecg_rectified_band_features_h1_kernel(
 
         load_x(0, 1)
         load_x(1, 1)
+        load_scale_rows(f_scales_first, filt_scales, slice(0, PASS))
+        load_x(2, 1)
+        load_x(3, 1)
         load_f_words(0)
-        load_scale_rows(f_scales_raw, filt_scales)
-        load_x(2, 2)
-        offset_sb = load_per_slot(offset, H_PASSES, "offset_sb")
         load_f_words(1)
+        offset_sb = load_per_slot(offset, H_PASSES, "offset_sb")
+        load_scale_rows(f_scales_rest, filt_scales, slice(PASS, H))
         load_f_words(2)
-        load_x(4, 4)
         s_words_raw = keep.tile([P, H_PASSES, 2 * N], U8, align_bytes=64)
         nc.sync.dma_start(
             out=s_words_raw[:].bitcast(I32), in_=smooth_words.rearrange("g p c -> p g c").bitcast(I32)
         )
-        load_scale_rows(s_scales_raw, smooth_scales)
+        load_scale_rows(s_scales_raw, smooth_scales, slice(0, N))
+        load_x(4, 4)
         base_sb = load_per_slot(base, 1, "base_sb")
         gain_sb = load_per_slot(gain, 1, "gain_sb")
         load_x(8, 4)
         load_x(12, 4)
 
-        def sort_columns(words_raw, scales_raw, passes, name):
-            words = keep.tile([P, PACK, passes, 2 * P], U8, name=name + "_words", align_bytes=64)
-            scales = keep.tile([P, PACK, passes, P], U8, name=name + "_scales", align_bytes=64)
+        def sort_words(raw, passes, name):
+            words = keep.tile([P, PACK, passes, 2 * P], U8, name=name, align_bytes=64)
             nc.vector.tensor_copy(
                 out=words[:].rearrange("p t g (m b) -> p t g m b", b=2),
-                in_=words_raw.rearrange("p g (m t b) -> p t g m b", t=PACK, b=2),
+                in_=raw.rearrange("p g (m t b) -> p t g m b", t=PACK, b=2),
             )
-            nc.vector.tensor_copy(out=scales[:], in_=scales_raw.rearrange("p g (m t) -> p t g m", t=PACK))
-            return words, scales
+            return words
 
-        f_sorted = {}
+        def sort_scales(raw, passes, name):
+            scales = keep.tile([P, PACK, passes, P], U8, name=name, align_bytes=64)
+            nc.vector.tensor_copy(out=scales[:], in_=raw.rearrange("p g (m t) -> p t g m", t=PACK))
+            return scales
 
-        def sort_f(hg):
-            f_sorted[hg] = sort_columns(
-                f_words_raw[hg][:], f_scales_raw[:, :, PASS * hg : PASS * (hg + 1)], K_PASSES, "f%d" % hg
-            )
+        f_words = {}
+        f_scales = {}
+        s_sorted = {}
+
+        def sort_f_words(hg):
+            f_words[hg] = sort_words(f_words_raw[hg][:], K_PASSES, "f%d_words" % hg)
+
+        def sort_f_scales(hg):
+            f_scales[hg] = sort_scales(f_scales_raw[hg], K_PASSES, "f%d_scales" % hg)
 
         x_grouped = {}
         x_mx = {}
 
-        def transpose_x(j):
-            for a in range(TILES):
-                words = x_rows[TILES * j + a].bitcast(F32)
+        def transpose_x(j, first, count):
+            chunk = work.tile([P, K_PASSES, count * P, 2], F32, name="x_chunk", bufs=4, align_bytes=64)
+            for a in range(count):
+                words = x_rows[TILES * j + first + a].bitcast(F32)
                 bank = next_bank()
                 quarters = bank[:].rearrange("p (g u r) -> p g u r", g=K_PASSES, u=2)
                 for g in range(K_PASSES):
@@ -138,53 +149,74 @@ def tile_ecg_rectified_band_features_h1_kernel(
                         nc.tensor.transpose(
                             quarters[:, g, u, :], words[:, 256 * g + u : 256 * (g + 1) : 2], ident[:]
                         )
-                if a % 2 == 0:
-                    half = work.tile([P, K_PASSES, 2 * P, 2], F32, name="x_half", bufs=4, align_bytes=64)
-                    x_grouped[j, a // 2] = half
-                nc.scalar.copy(
-                    out=half[:, :, P * (a % 2) : P * (a % 2 + 1), :], in_=quarters.rearrange("p g u r -> p g r u")
-                )
+                nc.scalar.copy(out=chunk[:, :, P * a : P * (a + 1), :], in_=quarters.rearrange("p g u r -> p g r u"))
+            x_grouped[j, first] = chunk
 
-        def quantize_x(j):
-            codes = work.tile([P, K_PASSES, GROUP], U32, name="x_codes", bufs=2, align_bytes=64)
-            scales = work.tile([P, K_PASSES, GROUP], U8, name="x_scales", bufs=2, align_bytes=64)
-            for h in range(2):
-                cols = slice(2 * P * h, 2 * P * (h + 1))
-                for g in range(K_PASSES):
-                    nc.vector.quantize_mx(
-                        out=codes[:, g, cols].bitcast(FP8X4),
-                        scales=scales[:, g, cols],
-                        in_=x_grouped[j, h][:, g, :, :].rearrange("p r u -> p (r u)").bitcast(BF16),
+        def transpose_x_group(j):
+            chunk = work.tile([P, K_PASSES, GROUP, 2], F32, name="x_chunk", bufs=4, align_bytes=64)
+            for g in range(K_PASSES):
+                for pair in range(TILES // 2):
+                    bank = next_bank()
+                    quarters = bank[:].rearrange("p (a u r) -> p a u r", a=2, u=2)
+                    for a in range(2):
+                        words = x_rows[TILES * j + 2 * pair + a].bitcast(F32)
+                        for u in range(2):
+                            nc.tensor.transpose(
+                                quarters[:, a, u, :], words[:, 256 * g + u : 256 * (g + 1) : 2], ident[:]
+                            )
+                    nc.scalar.copy(
+                        out=chunk[:, g, 2 * P * pair : 2 * P * (pair + 1), :].rearrange("p (a r) u -> p a r u", a=2),
+                        in_=quarters.rearrange("p a u r -> p a r u"),
                     )
-            x_mx[j] = (codes, scales)
+            x_grouped[j, 0] = chunk
+
+        def quantize_x(j, first, count):
+            if first == 0:
+                codes = work.tile([P, K_PASSES, GROUP], U32, name="x_codes", bufs=2, align_bytes=64)
+                scales = work.tile([P, K_PASSES, GROUP], U8, name="x_scales", bufs=2, align_bytes=64)
+                x_mx[j] = (codes, scales)
+            codes, scales = x_mx[j]
+            cols = slice(P * first, P * (first + count))
+            for g in range(K_PASSES):
+                nc.vector.quantize_mx(
+                    out=codes[:, g, cols].bitcast(FP8X4),
+                    scales=scales[:, g, cols],
+                    in_=x_grouped[j, first][:, g, :, :].rearrange("p r u -> p (r u)").bitcast(BF16),
+                )
 
         r_rows = {}
         r_grouped = {}
         r_mx = {}
 
-        def filter_bank(j, hg):
-            words, w_scales = f_sorted[hg]
+        def filter_passes(bank, j, hg, t, cols):
+            words, w_scales = f_words[hg], f_scales[hg]
             codes, scales = x_mx[j]
-            rows = work.tile([P, PACK, GROUP], BF16, name="r_rows", align_bytes=64)
+            for g in range(K_PASSES):
+                nc.tensor.matmul_mx(
+                    out=bank[:, cols],
+                    lhsT=words[:, t, g, :].bitcast(FP4X4),
+                    lhsT_scale=w_scales[:, t, g, :],
+                    rhs=codes[:, g, cols].bitcast(FP8X4),
+                    rhs_scale=scales[:, g, cols],
+                    start=(g == 0),
+                    stop=(g == K_PASSES - 1),
+                )
+
+        def rectify(bank, j, hg, t):
+            if t == 0:
+                r_rows[j, hg] = work.tile([P, PACK, GROUP], BF16, name="r_rows", align_bytes=64)
+            nc.scalar.activation(
+                out=r_rows[j, hg][:, t, :], in_=bank[:], func=ACT.Abs, bias=offset_sb[:, hg, t : t + 1]
+            )
+
+        def filter_bank(j, hg):
             for t in range(PACK):
                 bank = next_bank()
-                for g in range(K_PASSES):
-                    nc.tensor.matmul_mx(
-                        out=bank[:],
-                        lhsT=words[:, t, g, :].bitcast(FP4X4),
-                        lhsT_scale=w_scales[:, t, g, :],
-                        rhs=codes[:, g, :].bitcast(FP8X4),
-                        rhs_scale=scales[:, g, :],
-                        start=(g == 0),
-                        stop=(g == K_PASSES - 1),
-                    )
-                nc.scalar.activation(
-                    out=rows[:, t, :], in_=bank[:], func=ACT.Abs, bias=offset_sb[:, hg, t : t + 1]
-                )
-            r_rows[j, hg] = rows
+                filter_passes(bank, j, hg, t, slice(0, GROUP))
+                rectify(bank, j, hg, t)
 
-        def interleave(rows, name):
-            grouped = work.tile([P, GROUP, PACK], BF16, name=name, align_bytes=64)
+        def interleave(rows, width, name):
+            grouped = work.tile([P, width, PACK], BF16, name=name, align_bytes=64)
             nc.vector.tensor_copy(
                 out=grouped[:].rearrange("p (c i) t -> p c t i", i=RUN),
                 in_=rows[:].rearrange("p t (c i) -> p c t i", i=RUN),
@@ -192,11 +224,11 @@ def tile_ecg_rectified_band_features_h1_kernel(
             return grouped
 
         def interleave_r(j, hg):
-            r_grouped[j, hg] = interleave(r_rows[j, hg], "r_grouped")
+            r_grouped[j, hg] = interleave(r_rows[j, hg], GROUP, "r_grouped")
 
         def quantize_r(j, hg):
-            codes = work.tile([P, GROUP], U32, name="r_codes", bufs=4, align_bytes=64)
-            scales = work.tile([P, GROUP], U8, name="r_scales", bufs=4, align_bytes=64)
+            codes = work.tile([P, GROUP], U32, name="r_codes", bufs=6, align_bytes=64)
+            scales = work.tile([P, GROUP], U8, name="r_scales", bufs=6, align_bytes=64)
             nc.vector.quantize_mx(
                 out=codes[:].bitcast(FP8X4),
                 scales=scales[:],
@@ -206,44 +238,61 @@ def tile_ecg_rectified_band_features_h1_kernel(
 
         e_banks = {}
 
-        def smooth(j):
-            words, w_scales = s_sorted[0]
+        def smooth(j, order):
+            words, w_scales = s_sorted["words"], s_sorted["scales"]
             banks = [next_bank() for t in range(PACK)]
-            for hg in range(H_PASSES):
+            for t, hg in order:
                 codes, scales = r_mx[j, hg]
-                for t in range(PACK):
-                    nc.tensor.matmul_mx(
-                        out=banks[t][:],
-                        lhsT=words[:, t, hg, :].bitcast(FP4X4),
-                        lhsT_scale=w_scales[:, t, hg, :],
-                        rhs=codes[:].bitcast(FP8X4),
-                        rhs_scale=scales[:],
-                        start=(hg == 0),
-                        stop=(hg == H_PASSES - 1),
-                    )
+                nc.tensor.matmul_mx(
+                    out=banks[t][:],
+                    lhsT=words[:, t, hg, :].bitcast(FP4X4),
+                    lhsT_scale=w_scales[:, t, hg, :],
+                    rhs=codes[:].bitcast(FP8X4),
+                    rhs_scale=scales[:],
+                    start=(hg == 0),
+                    stop=(hg == H_PASSES - 1),
+                )
             e_banks[j] = banks
 
         y_rows = {}
         y_scales = keep.tile([P, M], U8, align_bytes=64)
 
-        def features(j):
-            root = work.tile([P, PACK, GROUP], F32, name="root", bufs=2)
-            rows = work.tile([P, PACK, GROUP], F32, name="y_rows", bufs=2)
+        roots = {}
+        y_grouped = {}
+
+        def square_roots(j, first, count):
+            cols = slice(P * first, P * (first + count))
+            root = work.tile([P, PACK, count * P], F32, name="root", bufs=2)
             for t in range(PACK):
                 nc.scalar.activation(
-                    out=root[:, t, :], in_=e_banks[j][t][:], func=ACT.Sqrt, bias=base_sb[:, 0, t : t + 1]
+                    out=root[:, t, :], in_=e_banks[j][t][:, cols], func=ACT.Sqrt, bias=base_sb[:, 0, t : t + 1]
                 )
-                nc.vector.tensor_scalar(
-                    out=rows[:, t, :], in0=root[:, t, :], scalar1=gain_sb[:, 0, t : t + 1], scalar2=None, op0=ALU.mult
-                )
-            y_rows[j] = rows
+            roots[j, first] = root
 
-        def planes(j):
-            cols = slice(GROUP * j, GROUP * (j + 1))
-            grouped = interleave(y_rows[j], "y_grouped")
-            codes = work.tile([P, GROUP], U32, name="y_codes", bufs=2, align_bytes=64)
+        def apply_gain(j, first, count, slots):
+            if 0 in slots:
+                rows = work.tile([P, PACK, count * P], F32, name="y_rows", bufs=3)
+                for a in range(count):
+                    y_rows[j, first + a] = (rows, a)
+            for t in slots:
+                nc.vector.tensor_scalar(
+                    out=y_rows[j, first][0][:, t, :],
+                    in0=roots[j, first][:, t, :],
+                    scalar1=gain_sb[:, 0, t : t + 1],
+                    scalar2=None,
+                    op0=ALU.mult,
+                )
+
+        def interleave_y(j, first, count):
+            y_grouped[j, first] = interleave(y_rows[j, first][0], count * P, "y_grouped")
+
+        def planes(j, first, count):
+            cols = slice(GROUP * j + P * first, GROUP * j + P * (first + count))
+            codes = work.tile([P, count * P], U32, name="y_codes", bufs=3, align_bytes=64)
             nc.vector.quantize_mx(
-                out=codes[:].bitcast(FP8X4), scales=y_scales[:, cols], in_=grouped[:].rearrange("p c t -> p (c t)")
+                out=codes[:].bitcast(FP8X4),
+                scales=y_scales[:, cols],
+                in_=y_grouped[j, first][:].rearrange("p c t -> p (c t)"),
             )
             nc.sync.dma_start(
                 out=out_1[0, :, cols, :].rearrange("p m t -> p (m t)").bitcast(I32), in_=codes[:].bitcast(I32)
@@ -258,62 +307,99 @@ def tile_ecg_rectified_band_features_h1_kernel(
 
         y_banks = {}
 
-        def transpose_y(j):
-            banks = [next_bank() for a in range(TILES)]
-            for a in range(TILES):
+        def transpose_y(j, tiles):
+            for a in tiles:
+                rows, place = y_rows[j, a]
+                bank = next_bank()
                 for t in range(PACK):
-                    nc.tensor.transpose(
-                        banks[a][:, P * t : P * (t + 1)], y_rows[j][:, t, P * a : P * (a + 1)], ident[:]
-                    )
-            y_banks[j] = banks
+                    nc.tensor.transpose(bank[:, P * t : P * (t + 1)], rows[:, t, P * place : P * (place + 1)], ident[:])
+                y_banks[j, a] = bank
 
-        def store_y(j, copies):
-            for a in range(TILES):
+        def store_y(j, tiles, copy):
+            for a in tiles:
                 result = work.tile([P, N], F32, name="y_out", bufs=4)
-                copies[a](
+                copy(
                     out=result[:].rearrange("p (m t) -> p m t", t=PACK),
-                    in_=y_banks[j][a][:].rearrange("p (t m) -> p m t", t=PACK),
+                    in_=y_banks[j, a][:].rearrange("p (t m) -> p m t", t=PACK),
                 )
                 row0 = GROUP * j + P * a
                 nc.sync.dma_start(out=out_0[row0 : row0 + P, :], in_=result[:])
 
-        on_vector = [nc.vector.tensor_copy] * TILES
-        shared = [nc.vector.tensor_copy, nc.scalar.copy] * (TILES // 2)
-        s_sorted = []
-        transpose_x(0)
-        sort_f(0)
-        quantize_x(0)
-        sort_f(1)
-        sort_f(2)
+        on_scalar, on_vector = nc.scalar.copy, nc.vector.tensor_copy
+        two_first = [(t, hg) for hg in range(H_PASSES) for t in range(2)]
+        by_slot = two_first + [(t, hg) for t in range(2, PACK) for hg in range(H_PASSES)]
+        by_pass = [(t, hg) for hg in range(H_PASSES) for t in range(PACK)]
         last = GROUPS - 1
-        for j in range(GROUPS):
+
+        for a in range(TILES):
+            transpose_x(0, a, 1)
+        sort_f_scales(0)
+        quantize_x(0, 0, 1)
+        quantize_x(0, 1, 1)
+        sort_f_words(0)
+        quantize_x(0, 2, 1)
+        quantize_x(0, 3, 1)
+        sort_f_words(1)
+        sort_f_scales(1)
+        filter_bank(0, 0)
+        sort_f_words(2)
+        sort_f_scales(2)
+        filter_bank(0, 1)
+        s_sorted["words"] = sort_words(s_words_raw[:], H_PASSES, "s_words")
+        interleave_r(0, 0)
+        s_sorted["scales"] = sort_scales(s_scales_raw[:], H_PASSES, "s_scales")
+        transpose_x_group(1)
+        interleave_r(0, 1)
+        quantize_r(0, 0)
+        filter_bank(0, 2)
+        quantize_x(1, 0, TILES)
+        quantize_r(0, 1)
+        interleave_r(0, 2)
+        quantize_r(0, 2)
+
+        for j in range(1, GROUPS):
             filter_bank(j, 0)
-            filter_bank(j, 1)
+            smooth(j - 1, by_slot)
+            square_roots(j - 1, 0, TILES)
             interleave_r(j, 0)
-            if j == 0:
-                s_sorted.append(sort_columns(s_words_raw[:], s_scales_raw[:], H_PASSES, "s"))
-            elif j < last:
-                transpose_y(j - 1)
-                store_y(j - 1, on_vector)
-            filter_bank(j, 2)
+            apply_gain(j - 1, 0, TILES, [0])
             quantize_r(j, 0)
+            apply_gain(j - 1, 0, TILES, [1, 2, 3])
+            filter_bank(j, 1)
+            interleave_y(j - 1, 0, TILES)
+            planes(j - 1, 0, TILES)
+            if j < last:
+                transpose_x_group(j + 1)
             interleave_r(j, 1)
-            if j < last:
-                transpose_x(j + 1)
-            else:
-                transpose_y(j - 1)
-            interleave_r(j, 2)
             quantize_r(j, 1)
-            quantize_r(j, 2)
-            if j == last:
-                store_y(j - 1, on_vector)
-                store_scale_rows(slice(0, GROUP * last))
-            smooth(j)
+            filter_bank(j, 2)
             if j < last:
-                quantize_x(j + 1)
-            features(j)
-            if j == last:
-                transpose_y(j)
-            planes(j)
-        store_y(last, [nc.scalar.copy] * TILES)
+                quantize_x(j + 1, 0, TILES)
+            interleave_r(j, 2)
+            transpose_y(j - 1, range(TILES))
+            if j < last:
+                store_y(j - 1, [0, 1], on_scalar)
+                store_y(j - 1, [2], on_vector)
+                quantize_r(j, 2)
+                store_y(j - 1, [3], on_vector)
+            else:
+                quantize_r(j, 2)
+                store_scale_rows(slice(0, GROUP * last))
+                store_y(j - 1, [0, 1], on_scalar)
+                store_y(j - 1, [2, 3], on_vector)
+        smooth(last, by_pass)
+        half = TILES // 2
+        square_roots(last, 0, half)
+        square_roots(last, half, half)
+        apply_gain(last, 0, half, range(PACK))
+        transpose_y(last, [0, 1])
+        interleave_y(last, 0, half)
+        apply_gain(last, half, half, range(PACK))
+        transpose_y(last, [2, 3])
+        store_y(last, [0, 1], on_scalar)
+        planes(last, 0, half)
+        interleave_y(last, half, half)
+        store_y(last, [2], on_scalar)
+        planes(last, half, half)
+        store_y(last, [3], on_scalar)
         store_scale_rows(slice(GROUP * last, M))

@@ -101,12 +101,12 @@ def tile_ecg_rectified_band_features_h1_kernel(
         offset_sb = load_per_slot(offset, H_PASSES, "offset_sb")
         load_scale_rows(f_scales_rest, filt_scales, slice(PASS, H))
         load_f_words(2)
+        load_x(4, 4)
         s_words_raw = keep.tile([P, H_PASSES, 2 * N], U8, align_bytes=64)
         nc.sync.dma_start(
             out=s_words_raw[:].bitcast(I32), in_=smooth_words.rearrange("g p c -> p g c").bitcast(I32)
         )
         load_scale_rows(s_scales_raw, smooth_scales, slice(0, N))
-        load_x(4, 4)
         base_sb = load_per_slot(base, 1, "base_sb")
         gain_sb = load_per_slot(gain, 1, "gain_sb")
         load_x(8, 4)
@@ -152,9 +152,11 @@ def tile_ecg_rectified_band_features_h1_kernel(
                 nc.scalar.copy(out=chunk[:, :, P * a : P * (a + 1), :], in_=quarters.rearrange("p g u r -> p g r u"))
             x_grouped[j, first] = chunk
 
-        def transpose_x_group(j):
-            chunk = work.tile([P, K_PASSES, GROUP, 2], F32, name="x_chunk", bufs=4, align_bytes=64)
-            for g in range(K_PASSES):
+        def transpose_x_group(j, passes):
+            if 0 in passes:
+                x_grouped[j, 0] = work.tile([P, K_PASSES, GROUP, 2], F32, name="x_chunk", bufs=4, align_bytes=64)
+            chunk = x_grouped[j, 0]
+            for g in passes:
                 for pair in range(TILES // 2):
                     bank = next_bank()
                     quarters = bank[:].rearrange("p (a u r) -> p a u r", a=2, u=2)
@@ -168,16 +170,15 @@ def tile_ecg_rectified_band_features_h1_kernel(
                         out=chunk[:, g, 2 * P * pair : 2 * P * (pair + 1), :].rearrange("p (a r) u -> p a r u", a=2),
                         in_=quarters.rearrange("p a u r -> p a r u"),
                     )
-            x_grouped[j, 0] = chunk
 
-        def quantize_x(j, first, count):
-            if first == 0:
+        def quantize_x(j, first, count, passes):
+            if first == 0 and 0 in passes:
                 codes = work.tile([P, K_PASSES, GROUP], U32, name="x_codes", bufs=2, align_bytes=64)
                 scales = work.tile([P, K_PASSES, GROUP], U8, name="x_scales", bufs=2, align_bytes=64)
                 x_mx[j] = (codes, scales)
             codes, scales = x_mx[j]
             cols = slice(P * first, P * (first + count))
-            for g in range(K_PASSES):
+            for g in passes:
                 nc.vector.quantize_mx(
                     out=codes[:, g, cols].bitcast(FP8X4),
                     scales=scales[:, g, cols],
@@ -334,25 +335,27 @@ def tile_ecg_rectified_band_features_h1_kernel(
         for a in range(TILES):
             transpose_x(0, a, 1)
         sort_f_scales(0)
-        quantize_x(0, 0, 1)
-        quantize_x(0, 1, 1)
+        quantize_x(0, 0, 1, [0, 1])
+        quantize_x(0, 1, 1, [0, 1])
         sort_f_words(0)
-        quantize_x(0, 2, 1)
-        quantize_x(0, 3, 1)
+        quantize_x(0, 2, 1, [0, 1])
+        quantize_x(0, 3, 1, [0, 1])
         sort_f_words(1)
         sort_f_scales(1)
         filter_bank(0, 0)
         sort_f_words(2)
         sort_f_scales(2)
+        transpose_x_group(1, [0])
         filter_bank(0, 1)
         s_sorted["words"] = sort_words(s_words_raw[:], H_PASSES, "s_words")
         interleave_r(0, 0)
         s_sorted["scales"] = sort_scales(s_scales_raw[:], H_PASSES, "s_scales")
-        transpose_x_group(1)
-        interleave_r(0, 1)
+        transpose_x_group(1, [1])
         quantize_r(0, 0)
+        quantize_x(1, 0, TILES, [0])
+        interleave_r(0, 1)
         filter_bank(0, 2)
-        quantize_x(1, 0, TILES)
+        quantize_x(1, 0, TILES, [1])
         quantize_r(0, 1)
         interleave_r(0, 2)
         quantize_r(0, 2)
@@ -365,16 +368,20 @@ def tile_ecg_rectified_band_features_h1_kernel(
             apply_gain(j - 1, 0, TILES, [0])
             quantize_r(j, 0)
             apply_gain(j - 1, 0, TILES, [1, 2, 3])
+            if j < last:
+                transpose_x_group(j + 1, [0])
             filter_bank(j, 1)
             interleave_y(j - 1, 0, TILES)
+            if j < last:
+                quantize_x(j + 1, 0, TILES, [0])
             planes(j - 1, 0, TILES)
             if j < last:
-                transpose_x_group(j + 1)
+                transpose_x_group(j + 1, [1])
             interleave_r(j, 1)
+            if j < last:
+                quantize_x(j + 1, 0, TILES, [1])
             quantize_r(j, 1)
             filter_bank(j, 2)
-            if j < last:
-                quantize_x(j + 1, 0, TILES)
             interleave_r(j, 2)
             transpose_y(j - 1, range(TILES))
             if j < last:
@@ -388,18 +395,18 @@ def tile_ecg_rectified_band_features_h1_kernel(
                 store_y(j - 1, [0, 1], on_scalar)
                 store_y(j - 1, [2, 3], on_vector)
         smooth(last, by_pass)
-        half = TILES // 2
-        square_roots(last, 0, half)
-        square_roots(last, half, half)
-        apply_gain(last, 0, half, range(PACK))
-        transpose_y(last, [0, 1])
-        interleave_y(last, 0, half)
-        apply_gain(last, half, half, range(PACK))
-        transpose_y(last, [2, 3])
-        store_y(last, [0, 1], on_scalar)
-        planes(last, 0, half)
-        interleave_y(last, half, half)
+        square_roots(last, 0,2)
+        square_roots(last, 2,2)
+        apply_gain(last, 0,2, range(PACK))
+        transpose_y(last, [0,1])
+        interleave_y(last, 0,2)
+        apply_gain(last, 2,2, range(PACK))
+        transpose_y(last, [2,3])
+        store_y(last, [0], on_scalar)
+        store_y(last, [1], on_scalar)
+        planes(last, 0,2)
+        interleave_y(last, 2,2)
         store_y(last, [2], on_scalar)
-        planes(last, half, half)
+        planes(last, 2,2)
         store_y(last, [3], on_scalar)
         store_scale_rows(slice(GROUP * last, M))

@@ -152,6 +152,22 @@ def tile_ecg_rectified_band_features_h1_kernel(
                 nc.scalar.copy(out=chunk[:, :, P * a : P * (a + 1), :], in_=quarters.rearrange("p g u r -> p g r u"))
             x_grouped[j, first] = chunk
 
+        x_sorted = {}
+
+        def sort_x(j, copy):
+            for a in range(TILES):
+                words = work.tile([P, K_PASSES, 2, P], F32, name="x_sorted", bufs=4)
+                copy(
+                    out=words[:],
+                    in_=x_rows[TILES * j + a].bitcast(F32).rearrange("p (g m u) -> p g u m", g=K_PASSES, u=2),
+                )
+                x_sorted[j, a] = words
+
+        def x_words(j, a, g, u):
+            if (j, a) in x_sorted:
+                return x_sorted[j, a][:, g, u, :]
+            return x_rows[TILES * j + a].bitcast(F32)[:, 2 * P * g + u : 2 * P * (g + 1) : 2]
+
         def transpose_x_group(j, passes):
             if 0 in passes:
                 x_grouped[j, 0] = work.tile([P, K_PASSES, GROUP, 2], F32, name="x_chunk", bufs=4, align_bytes=64)
@@ -161,11 +177,8 @@ def tile_ecg_rectified_band_features_h1_kernel(
                     bank = next_bank()
                     quarters = bank[:].rearrange("p (a u r) -> p a u r", a=2, u=2)
                     for a in range(2):
-                        words = x_rows[TILES * j + 2 * pair + a].bitcast(F32)
                         for u in range(2):
-                            nc.tensor.transpose(
-                                quarters[:, a, u, :], words[:, 256 * g + u : 256 * (g + 1) : 2], ident[:]
-                            )
+                            nc.tensor.transpose(quarters[:, a, u, :], x_words(j, 2 * pair + a, g, u), ident[:])
                     nc.scalar.copy(
                         out=chunk[:, g, 2 * P * pair : 2 * P * (pair + 1), :].rearrange("p (a r) u -> p a r u", a=2),
                         in_=quarters.rearrange("p a u r -> p a r u"),
@@ -362,26 +375,24 @@ def tile_ecg_rectified_band_features_h1_kernel(
 
         for j in range(1, GROUPS):
             filter_bank(j, 0)
+            if j < last:
+                sort_x(j + 1, on_vector)
             smooth(j - 1, by_slot)
             square_roots(j - 1, 0, TILES)
             interleave_r(j, 0)
             apply_gain(j - 1, 0, TILES, [0])
             quantize_r(j, 0)
             apply_gain(j - 1, 0, TILES, [1, 2, 3])
-            if j < last:
-                transpose_x_group(j + 1, [0])
             filter_bank(j, 1)
             interleave_y(j - 1, 0, TILES)
-            if j < last:
-                quantize_x(j + 1, 0, TILES, [0])
             planes(j - 1, 0, TILES)
             if j < last:
-                transpose_x_group(j + 1, [1])
+                transpose_x_group(j + 1, [0, 1])
             interleave_r(j, 1)
-            if j < last:
-                quantize_x(j + 1, 0, TILES, [1])
             quantize_r(j, 1)
             filter_bank(j, 2)
+            if j < last:
+                quantize_x(j + 1, 0, TILES, [0, 1])
             interleave_r(j, 2)
             transpose_y(j - 1, range(TILES))
             if j < last:

from contextlib import ExitStack

import concourse.mybir as mybir
from concourse.masks import make_identity

M, K, H, N = 2048, 1024, 1536, 512
FLOPS = 2 * M * K * H + 2 * M * H * N

F32 = mybir.dt.float32
BF16 = mybir.dt.bfloat16
I32 = mybir.dt.int32
U32 = mybir.dt.uint32
U8 = mybir.dt.uint8
FP8X4 = mybir.dt.float8_e4m3fn_x4
FP4X4 = mybir.dt.float4_e2m1fn_x4
ACT = mybir.ActivationFunctionType
ALU = mybir.AluOpType

P = 128
PACK = 4
PASS = P * PACK
GROUP = 512
GROUPS = M // GROUP
TILES = GROUP // P
K_PASSES = K // PASS
H_PASSES = H // PASS
BANKS = 8
RUN = 4


def tile_ecg_rectified_band_features_h1_kernel(
    tc, x, filt_words, filt_scales, offset, smooth_words, smooth_scales, base, gain, out_0, out_1, out_2
):
    nc = tc.nc
    with ExitStack() as ctx:
        keep = ctx.enter_context(tc.tile_pool(name="keep", bufs=1))
        work = ctx.enter_context(tc.tile_pool(name="work", bufs=3))
        psum = ctx.enter_context(tc.psum_pool(name="psum", bufs=1))
        ctx.enter_context(tc.manual_schedule())

        banks_taken = []

        def next_bank():
            index = len(banks_taken) % BANKS
            bank = psum.tile([P, GROUP], F32, name="bank%d" % index, tag="bank%d" % index)
            banks_taken.append(index)
            return bank

        f_scales_first = keep.tile([P, K_PASSES, PASS], U8, align_bytes=64)
        f_scales_rest = keep.tile([P, K_PASSES, H - PASS], U8, align_bytes=64)
        s_scales_raw = keep.tile([P, H_PASSES, N], U8, align_bytes=64)
        for plane in (f_scales_first, f_scales_rest, s_scales_raw):
            nc.vector.memset(plane[:].bitcast(I32), 0)
        f_scales_raw = [f_scales_first[:], f_scales_rest[:, :, :PASS], f_scales_rest[:, :, PASS:]]
        ident = keep.tile([P, P], F32)
        make_identity(nc, ident[:])
        warm_in = keep.tile([P, 1], F32)
        warm_out = keep.tile([P, 1], F32)
        nc.vector.memset(warm_in[:], 1.0)
        nc.scalar.activation(out=warm_out[:], in_=warm_in[:], func=ACT.Sqrt)

        def load_scale_rows(tile, rows, cols):
            for q in range(4):
                nc.sync.dma_start(
                    out=tile[32 * q : 32 * q + 4, :, :].bitcast(I32),
                    in_=rows[:, 4 * q : 4 * q + 4, cols].rearrange("g r n -> r g n").bitcast(I32),
                )

        f_words_raw = {}

        def load_f_words(hg):
            raw = keep.tile([P, K_PASSES, 2 * PASS], U8, name="f_raw%d" % hg, align_bytes=64)
            nc.sync.dma_start(
                out=raw[:].bitcast(I32),
                in_=filt_words[:, :, 2 * PASS * hg : 2 * PASS * (hg + 1)].rearrange("g p c -> p g c").bitcast(I32),
            )
            f_words_raw[hg] = raw

        x_rows = {}

        def load_x(first, count):
            rows = keep.tile([P, count, K], BF16, name="x%d" % first, align_bytes=64)
            nc.sync.dma_start(
                out=rows[:], in_=x[P * first : P * (first + count), :].rearrange("(a p) k -> p a k", p=P)
            )
            for a in range(count):
                x_rows[first + a] = rows[:, a, :]

        def load_per_slot(vec, passes, name):
            tile = keep.tile([P, passes, PACK], BF16, name=name)
            nc.sync.dma_start(out=tile[:], in_=vec.rearrange("(g p t) -> p g t", p=P, t=PACK))
            return tile

        load_x(0, 1)
        load_x(1, 1)
        load_scale_rows(f_scales_first, filt_scales, slice(0, PASS))
        load_x(2, 1)
        load_x(3, 1)
        load_f_words(0)
        load_f_words(1)
        offset_sb = load_per_slot(offset, H_PASSES, "offset_sb")
        load_scale_rows(f_scales_rest, filt_scales, slice(PASS, H))
        load_f_words(2)
        load_x(4, 4)
        s_words_raw = keep.tile([P, H_PASSES, 2 * N], U8, align_bytes=64)
        nc.sync.dma_start(
            out=s_words_raw[:].bitcast(I32), in_=smooth_words.rearrange("g p c -> p g c").bitcast(I32)
        )
        load_scale_rows(s_scales_raw, smooth_scales, slice(0, N))
        base_sb = load_per_slot(base, 1, "base_sb")
        gain_sb = load_per_slot(gain, 1, "gain_sb")
        load_x(8, 4)
        load_x(12, 4)

        def sort_words(raw, passes, name):
            words = keep.tile([P, PACK, passes, 2 * P], U8, name=name, align_bytes=64)
            nc.vector.tensor_copy(
                out=words[:].rearrange("p t g (m b) -> p t g m b", b=2),
                in_=raw.rearrange("p g (m t b) -> p t g m b", t=PACK, b=2),
            )
            return words

        def sort_scales(raw, passes, name):
            scales = keep.tile([P, PACK, passes, P], U8, name=name, align_bytes=64)
            nc.vector.tensor_copy(out=scales[:], in_=raw.rearrange("p g (m t) -> p t g m", t=PACK))
            return scales

        f_words = {}
        f_scales = {}
        s_sorted = {}

        def sort_f_words(hg):
            f_words[hg] = sort_words(f_words_raw[hg][:], K_PASSES, "f%d_words" % hg)

        def sort_f_scales(hg):
            f_scales[hg] = sort_scales(f_scales_raw[hg], K_PASSES, "f%d_scales" % hg)

        x_grouped = {}
        x_mx = {}

        def transpose_x(j, first, count):
            chunk = work.tile([P, K_PASSES, count * P, 2], F32, name="x_chunk", bufs=4, align_bytes=64)
            for a in range(count):
                words = x_rows[TILES * j + first + a].bitcast(F32)
                bank = next_bank()
                quarters = bank[:].rearrange("p (g u r) -> p g u r", g=K_PASSES, u=2)
                for g in range(K_PASSES):
                    for u in range(2):
                        nc.tensor.transpose(
                            quarters[:, g, u, :], words[:, 256 * g + u : 256 * (g + 1) : 2], ident[:]
                        )
                nc.scalar.copy(out=chunk[:, :, P * a : P * (a + 1), :], in_=quarters.rearrange("p g u r -> p g r u"))
            x_grouped[j, first] = chunk

        x_sorted = {}

        def sort_x(j, copy):
            for a in range(TILES):
                words = work.tile([P, K_PASSES, 2, P], F32, name="x_sorted", bufs=4)
                copy(
                    out=words[:],
                    in_=x_rows[TILES * j + a].bitcast(F32).rearrange("p (g m u) -> p g u m", g=K_PASSES, u=2),
                )
                x_sorted[j, a] = words

        def x_words(j, a, g, u):
            if (j, a) in x_sorted:
                return x_sorted[j, a][:, g, u, :]
            return x_rows[TILES * j + a].bitcast(F32)[:, 2 * P * g + u : 2 * P * (g + 1) : 2]

        def transpose_x_group(j, passes):
            if 0 in passes:
                x_grouped[j, 0] = work.tile([P, K_PASSES, GROUP, 2], F32, name="x_chunk", bufs=4, align_bytes=64)
            chunk = x_grouped[j, 0]
            for g in passes:
                for pair in range(TILES // 2):
                    bank = next_bank()
                    quarters = bank[:].rearrange("p (a u r) -> p a u r", a=2, u=2)
                    for a in range(2):
                        for u in range(2):
                            nc.tensor.transpose(quarters[:, a, u, :], x_words(j, 2 * pair + a, g, u), ident[:])
                    nc.scalar.copy(
                        out=chunk[:, g, 2 * P * pair : 2 * P * (pair + 1), :].rearrange("p (a r) u -> p a r u", a=2),
                        in_=quarters.rearrange("p a u r -> p a r u"),
                    )

        def quantize_x(j, first, count, passes):
            if first == 0 and 0 in passes:
                codes = work.tile([P, K_PASSES, GROUP], U32, name="x_codes", bufs=2, align_bytes=64)
                scales = work.tile([P, K_PASSES, GROUP], U8, name="x_scales", bufs=2, align_bytes=64)
                x_mx[j] = (codes, scales)
            codes, scales = x_mx[j]
            cols = slice(P * first, P * (first + count))
            for g in passes:
                nc.vector.quantize_mx(
                    out=codes[:, g, cols].bitcast(FP8X4),
                    scales=scales[:, g, cols],
                    in_=x_grouped[j, first][:, g, :, :].rearrange("p r u -> p (r u)").bitcast(BF16),
                )

        r_rows = {}
        r_grouped = {}
        r_mx = {}

        def filter_passes(bank, j, hg, t, cols):
            words, w_scales = f_words[hg], f_scales[hg]
            codes, scales = x_mx[j]
            for g in range(K_PASSES):
                nc.tensor.matmul_mx(
                    out=bank[:, cols],
                    lhsT=words[:, t, g, :].bitcast(FP4X4),
                    lhsT_scale=w_scales[:, t, g, :],
                    rhs=codes[:, g, cols].bitcast(FP8X4),
                    rhs_scale=scales[:, g, cols],
                    start=(g == 0),
                    stop=(g == K_PASSES - 1),
                )

        def rectify(bank, j, hg, t):
            if t == 0:
                r_rows[j, hg] = work.tile([P, PACK, GROUP], BF16, name="r_rows", align_bytes=64)
            nc.scalar.activation(
                out=r_rows[j, hg][:, t, :], in_=bank[:], func=ACT.Abs, bias=offset_sb[:, hg, t : t + 1]
            )

        def filter_bank(j, hg):
            for t in range(PACK):
                bank = next_bank()
                filter_passes(bank, j, hg, t, slice(0, GROUP))
                rectify(bank, j, hg, t)

        def interleave(rows, width, name):
            grouped = work.tile([P, width, PACK], BF16, name=name, align_bytes=64)
            nc.vector.tensor_copy(
                out=grouped[:].rearrange("p (c i) t -> p c t i", i=RUN),
                in_=rows[:].rearrange("p t (c i) -> p c t i", i=RUN),
            )
            return grouped

        def interleave_r(j, hg):
            r_grouped[j, hg] = interleave(r_rows[j, hg], GROUP, "r_grouped")

        def quantize_r(j, hg):
            codes = work.tile([P, GROUP], U32, name="r_codes", bufs=6, align_bytes=64)
            scales = work.tile([P, GROUP], U8, name="r_scales", bufs=6, align_bytes=64)
            nc.vector.quantize_mx(
                out=codes[:].bitcast(FP8X4),
                scales=scales[:],
                in_=r_grouped[j, hg][:].rearrange("p c t -> p (c t)"),
            )
            r_mx[j, hg] = (codes, scales)

        e_banks = {}

        def smooth(j, order):
            words, w_scales = s_sorted["words"], s_sorted["scales"]
            banks = [next_bank() for t in range(PACK)]
            for t, hg in order:
                codes, scales = r_mx[j, hg]
                nc.tensor.matmul_mx(
                    out=banks[t][:],
                    lhsT=words[:, t, hg, :].bitcast(FP4X4),
                    lhsT_scale=w_scales[:, t, hg, :],
                    rhs=codes[:].bitcast(FP8X4),
                    rhs_scale=scales[:],
                    start=(hg == 0),
                    stop=(hg == H_PASSES - 1),
                )
            e_banks[j] = banks

        y_rows = {}
        y_scales = keep.tile([P, M], U8, align_bytes=64)

        roots = {}
        y_grouped = {}

        def square_roots(j, first, count):
            cols = slice(P * first, P * (first + count))
            root = work.tile([P, PACK, count * P], F32, name="root", bufs=2)
            for t in range(PACK):
                nc.scalar.activation(
                    out=root[:, t, :], in_=e_banks[j][t][:, cols], func=ACT.Sqrt, bias=base_sb[:, 0, t : t + 1]
                )
            roots[j, first] = root

        def apply_gain(j, first, count, slots):
            if 0 in slots:
                rows = work.tile([P, PACK, count * P], F32, name="y_rows", bufs=3)
                for a in range(count):
                    y_rows[j, first + a] = (rows, a)
            for t in slots:
                nc.vector.tensor_scalar(
                    out=y_rows[j, first][0][:, t, :],
                    in0=roots[j, first][:, t, :],
                    scalar1=gain_sb[:, 0, t : t + 1],
                    scalar2=None,
                    op0=ALU.mult,
                )

        def interleave_y(j, first, count):
            y_grouped[j, first] = interleave(y_rows[j, first][0], count * P, "y_grouped")

        def planes(j, first, count):
            cols = slice(GROUP * j + P * first, GROUP * j + P * (first + count))
            codes = work.tile([P, count * P], U32, name="y_codes", bufs=3, align_bytes=64)
            nc.vector.quantize_mx(
                out=codes[:].bitcast(FP8X4),
                scales=y_scales[:, cols],
                in_=y_grouped[j, first][:].rearrange("p c t -> p (c t)"),
            )
            nc.sync.dma_start(
                out=out_1[0, :, cols, :].rearrange("p m t -> p (m t)").bitcast(I32), in_=codes[:].bitcast(I32)
            )

        def store_scale_rows(cols):
            for q in range(4):
                nc.sync.dma_start(
                    out=out_2[0, 4 * q : 4 * q + 4, cols].bitcast(I32),
                    in_=y_scales[32 * q : 32 * q + 4, cols].bitcast(I32),
                )

        y_banks = {}

        def transpose_y(j, tiles):
            for a in tiles:
                rows, place = y_rows[j, a]
                bank = next_bank()
                for t in range(PACK):
                    nc.tensor.transpose(bank[:, P * t : P * (t + 1)], rows[:, t, P * place : P * (place + 1)], ident[:])
                y_banks[j, a] = bank

        def store_y(j, tiles, copy):
            for a in tiles:
                result = work.tile([P, N], F32, name="y_out", bufs=4)
                copy(
                    out=result[:].rearrange("p (m t) -> p m t", t=PACK),
                    in_=y_banks[j, a][:].rearrange("p (t m) -> p m t", t=PACK),
                )
                row0 = GROUP * j + P * a
                nc.sync.dma_start(out=out_0[row0 : row0 + P, :], in_=result[:])

        on_scalar, on_vector = nc.scalar.copy, nc.vector.tensor_copy
        two_first = [(t, hg) for hg in range(H_PASSES) for t in range(2)]
        by_slot = two_first + [(t, hg) for t in range(2, PACK) for hg in range(H_PASSES)]
        by_pass = [(t, hg) for hg in range(H_PASSES) for t in range(PACK)]
        last = GROUPS - 1

        for a in range(TILES):
            transpose_x(0, a, 1)
        sort_f_scales(0)
        quantize_x(0, 0, 1, [0, 1])
        quantize_x(0, 1, 1, [0, 1])
        sort_f_words(0)
        quantize_x(0, 2, 1, [0, 1])
        quantize_x(0, 3, 1, [0, 1])
        sort_f_words(1)
        sort_f_scales(1)
        filter_bank(0, 0)
        sort_f_words(2)
        sort_f_scales(2)
        transpose_x_group(1, [0])
        filter_bank(0, 1)
        s_sorted["words"] = sort_words(s_words_raw[:], H_PASSES, "s_words")
        interleave_r(0, 0)
        s_sorted["scales"] = sort_scales(s_scales_raw[:], H_PASSES, "s_scales")
        transpose_x_group(1, [1])
        quantize_r(0, 0)
        quantize_x(1, 0, TILES, [0])
        interleave_r(0, 1)
        filter_bank(0, 2)
        quantize_x(1, 0, TILES, [1])
        quantize_r(0, 1)
        interleave_r(0, 2)
        quantize_r(0, 2)

        for j in range(1, GROUPS):
            filter_bank(j, 0)
            if j < last:
                sort_x(j + 1, on_vector)
            smooth(j - 1, by_slot)
            square_roots(j - 1, 0, TILES)
            interleave_r(j, 0)
            apply_gain(j - 1, 0, TILES, [0])
            quantize_r(j, 0)
            apply_gain(j - 1, 0, TILES, [1, 2, 3])
            filter_bank(j, 1)
            interleave_y(j - 1, 0, TILES)
            planes(j - 1, 0, TILES)
            if j < last:
                transpose_x_group(j + 1, [0, 1])
            interleave_r(j, 1)
            quantize_r(j, 1)
            filter_bank(j, 2)
            if j < last:
                quantize_x(j + 1, 0, TILES, [0, 1])
            interleave_r(j, 2)
            transpose_y(j - 1, range(TILES))
            if j < last:
                store_y(j - 1, [0, 1], on_scalar)
                store_y(j - 1, [2], on_vector)
                quantize_r(j, 2)
                store_y(j - 1, [3], on_vector)
            else:
                quantize_r(j, 2)
                store_scale_rows(slice(0, GROUP * last))
                store_y(j - 1, [0, 1], on_scalar)
                store_y(j - 1, [2, 3], on_vector)
        smooth(last, by_pass)
        square_roots(last, 0,2)
        square_roots(last, 2,2)
        apply_gain(last, 0,2, range(PACK))
        transpose_y(last, [0,1])
        interleave_y(last, 0,2)
        apply_gain(last, 2,2, range(PACK))
        transpose_y(last, [2,3])
        store_y(last, [0], on_scalar)
        store_y(last, [1], on_scalar)
        planes(last, 0,2)
        interleave_y(last, 2,2)
        store_y(last, [2], on_scalar)
        planes(last, 2,2)
        store_y(last, [3], on_scalar)
        store_scale_rows(slice(GROUP * last, M))
